import numpy as np, ml_dtypes
CORES = [12,28,60,100,156,228]
N = 6
KB, QP = 4, 128
ROOT = 1
def setup_inputs(rng):
    q = rng.standard_normal((N, 128, QP), dtype=np.float32) / 4; k = rng.standard_normal((N, 128, KB * 128), dtype=np.float32)
    a = 2 * np.pi * rng.random((N, QP)); s = 400 * rng.random((N, QP)) ** 1.5; q[:, 0, :] = s * np.cos(a); q[:, 1, :] = s * np.sin(a); q[:, 2, :] = 150 * rng.standard_normal((N, QP)); k[:, 2, :] = 1 + k[:, 2, :] / 50
    a = (2 * np.pi * rng.random() + np.pi / 2 * (rng.permutation(N).reshape(N, 1, 1) + 0.5) / N - 0.5 + (np.arange(KB).reshape(1, KB, 1) + rng.random((N, KB, 128))) / KB).reshape(N, KB * 128); k[:, 0, :] = np.cos(a); k[:, 1, :] = np.sin(a)
    for t in range(0, QP, 2):
        j, i = (t // 2) % N, rng.integers(KB * 128); q[ROOT, :2, t] = s[ROOT, t] * k[j, :2, i]; q[ROOT, 3:, t] += k[j, 3:, i] / 8
    return {"q": q.astype(ml_dtypes.bfloat16), "k": k.astype(ml_dtypes.bfloat16), "v": rng.standard_normal((N, 128, KB * 128), dtype=np.float32).astype(ml_dtypes.bfloat16)}
def setup_inputs_big(rng):
    d = setup_inputs(rng)
    for k in ("v",): d[k] = (d[k].astype(np.float32) * 1048576.0).astype(d[k].dtype)
    return d
def setup_inputs_small(rng):
    d = setup_inputs(rng)
    for k in ("v",): d[k] = (d[k].astype(np.float32) * (1 / 1048576.0)).astype(d[k].dtype)
    return d
def reference(q, k, v):
    Q, K, V = q.astype(np.float64), k.astype(np.float64), v.astype(np.float64)
    y = np.full((N, QP, 128), np.nan)
    for r in [ROOT]:
        js = list(range(N))
        S = np.concatenate([K[j].T @ Q[r] for j in js], axis=0)
        P = np.exp(S - S.max(axis=0)); P = P / P.sum(axis=0)
        y[r] = P.T @ np.concatenate([V[j][:, 128 * b:128 * b + 128] for j in js for b in range(KB)], axis=0)
    return {"y": y.astype(ml_dtypes.bfloat16)}

@@ -1,0 +1,227 @@
+from concourse.bass import DstId, RemoteDMATransfer
+from concourse.mybir import AluOpType, AxisListType, ActivationFunctionType
+
+KB = 4
+W = 136
+PW = 130
+NSLOT = 7
+
+SCRATCH = {
+    "qs": ("sbuf", [128, 128], "bfloat16"),
+    "ks": ("sbuf", [128, 512], "bfloat16"),
+    "vs": ("sbuf", [128, KB, W], "bfloat16"),
+    "ramp": ("sbuf", [128, 128], "float32"),
+    "ident": ("sbuf", [128, 128], "bfloat16"),
+    "ones": ("sbuf", [128, 128], "bfloat16"),
+    "dg": ("sbuf", [128, 128], "bfloat16"),
+    "P": ("sbuf", [128, 512], "bfloat16"),
+    "pk": ("sbuf", [128, W], "bfloat16"),
+    "land": ("sbuf", [128, NSLOT * W], "bfloat16"),
+    "m1w": ("sbuf", [128, 4], "float32"),
+    "m2w": ("sbuf", [128, 4], "float32"),
+    "m1d": ("sbuf", [128, 512], "bfloat16"),
+    "m2d": ("sbuf", [128, 512], "bfloat16"),
+    "nM": ("sbuf", [128, 8], "bfloat16"),
+    "wl": ("sbuf", [128, 4], "float32"),
+    "L": ("sbuf", [128, 4], "float32"),
+    "ys": ("sbuf", [128, 128], "bfloat16"),
+    "ps": ("psum", [128, 8 * 512], "float32"),
+}
+SEMAPHORES = (["q", "k", "v", "vone", "ramp", "idn", "ones", "qarr", "karr", "varr", "sent", "st", "nm", "dg", "o", "pk",
+               "retA", "retB", "m1M", "m1w", "m1a", "m1done", "m2M", "m2w", "m2a", "wl", "L", "rL", "ys", "y"]
+              + ["sb%d" % b for b in range(KB)] + ["p%d" % b for b in range(KB)]
+              + ["m1d%d" % j for j in range(4)] + ["m2d%d" % j for j in range(4)])
+
+X = AxisListType.X
+ACT = ActivationFunctionType
+
+
+def engines(mask, n, skip=0):
+    bits = [i for i in range(mask.bit_length()) if (mask >> i) & 1][skip:skip + n]
+    return sum(1 << i for i in bits)
+
+
+def count(mask):
+    return bin(mask).count("1")
+
+
+def plan(T, topo):
+    root = T.cores[T.root]
+    world = (max(topo.host(c) for c in T.cores) + 1) * topo.CORES_PER_HOST
+
+    def neighbours(c):
+        return [x for x in range(world) if x not in T.cores and topo.host(x) == topo.host(c)
+                and topo.chip(x) == topo.chip(c) and topo.die(x) == topo.die(c)]
+
+    direct = [c for c in T.cores if c != root and topo.may_write(root, c) and topo.may_write(c, root)]
+    far = [c for c in T.cores if c != root and c not in direct]
+    proxy = [[x for x in neighbours(c) if topo.may_write(x, root)][0] for c in far]
+    helper = []
+    for p in proxy:
+        helper.append([x for x in neighbours(root) if topo.may_write(x, p) and x not in helper][0])
+    return root, direct, far, proxy, helper
+
+
+def constants(g, T):
+    S = T.sem
+    g.iota(T.ramp[:], [[-1, 128]], 0, 1, allow_small_or_imprecise_dtypes=True).then_inc(S.ramp, 1)
+    g.vector.wait_ge(S.ramp, 1)
+    g.vector.tensor_scalar(T.ident[:], T.ramp[:], 0.0, None, AluOpType.is_equal).then_inc(S.idn, 1)
+    g.scalar.wait_ge(S.ramp, 1)
+    g.scalar.activation(T.ones[:], T.ramp[:], ACT.Exp, scale=0.0).then_inc(S.ones, 1)
+
+
+def worker(g, T, q_ready, k_ready, v_ready, pk_o, pk_m):
+    S, ps = T.sem, T.ps
+    pe, dve, act = g.tensor, g.vector, g.scalar
+    ST = ps[:, 0:512]
+    SB = [ps[:, 512 * (1 + b):512 * (1 + b) + 128] for b in range(KB)]
+    O = ps[:, 512 * 5:512 * 5 + 129]
+    for s, n in q_ready + k_ready:
+        pe.wait_ge(s, n)
+    pe.matmul(ST, T.qs[:], T.ks[:], True, True).then_inc(S.st, 1)
+    for b in range(KB):
+        pe.matmul(SB[b], T.ks[:, 128 * b:128 * b + 128], T.qs[:], True, False)
+    dve.wait_ge(S.st, 1)
+    dve.tensor_reduce(pk_m, ST, X, AluOpType.max, negate=True).then_inc(S.nm, 1)
+    dve.wait_ge(S.nm, 1)
+    dve.wait_ge(S.idn, 1)
+    dve.tensor_scalar(T.dg[:], T.ident[:], pk_m, None, AluOpType.mult).then_inc(S.dg, 1)
+    pe.wait_ge(S.dg, 1)
+    pe.wait_ge(S.ones, 1)
+    for b in range(KB):
+        pe.matmul(SB[b], T.ones[:], T.dg[:], False, True).then_inc(S["sb%d" % b], 1)
+        act.wait_ge(S["sb%d" % b], 1)
+        act.activation(T.P[:, 128 * b:128 * b + 128], SB[b], ACT.Exp).then_inc(S["p%d" % b], 1)
+    for s, n in v_ready:
+        pe.wait_ge(s, n)
+    for b in range(KB):
+        pe.wait_ge(S["p%d" % b], 1)
+        mm = pe.matmul(O, T.P[:, 128 * b:128 * b + 128], T.vs[:, b, 0:129], b == 0, b == KB - 1)
+    mm.then_inc(S.o, 1)
+    dve.wait_ge(S.o, 1)
+    dve.tensor_copy(pk_o, O).then_inc(S.pk, 1)
+
+
+def merge(g, T, pre, lo, n, acc, ready, negM):
+    S, land = T.sem, T.land
+    pe, dve, act = g.tensor, g.vector, g.scalar
+    negm = land[:, W * lo + 129:W * (lo + n - 1) + 130:W]
+    w, d = T[pre + "w"], T[pre + "d"]
+    for s, v in ready:
+        dve.wait_ge(s, v)
+    dve.tensor_reduce(negM, negm, X, AluOpType.min).then_inc(S[pre + "M"], 1)
+    act.wait_ge(S[pre + "M"], 1)
+    act.activation(w[:, 0:n], negm, ACT.Exp, bias=negM, scale=-1.0).then_inc(S[pre + "w"], 1)
+    act.wait_ge(S[pre + "w"], 1)
+    for j in range(n):
+        act.activation(d[:, 128 * j:128 * j + 128], T.ident[:], ACT.Copy, scale=w[:, j:j + 1]).then_inc(S[pre + "d%d" % j], 1)
+        pe.wait_ge(S[pre + "d%d" % j], 1)
+        mm = pe.matmul(acc, d[:, 128 * j:128 * j + 128], land[:, W * (lo + j):W * (lo + j) + 129], j == 0, j == n - 1)
+    mm.then_inc(S[pre + "a"], 1)
+
+
+def rank_program(g, core, T, topo):
+    S = T.sem
+    root, direct, far, proxy, helper = plan(T, topo)
+    nf = len(far)
+    own_slot = 1 + nf
+
+    def send(dst, out, in_, sem, n, skip=0):
+        rid, pid = topo.addr(dst, core)
+        m = engines(topo.mask(core, dst), n, skip)
+        g.remote_dma(out_ap=out, in_ap=in_, remote_sem=sem, local_sem=S.sent, pid=pid, routing_id=rid, dma_engine_mask=m)
+        return count(m)
+
+    def load_v(queue):
+        g.vector.memset(T.vs[:, :, 128:W], 1.0).then_inc(S.vone, 1)
+        queue.dma_start(T.vs[:, :, 0:128], T.v[:, :]).then_inc(S.v, 16)
+
+    if core == root:
+        g.sync.dma_start(T.qs[:], T.q[:, :]).then_inc(S.q, 16)
+        constants(g, T)
+        g.wait_ge(S.q, 16)
+        tr, left = [], 0
+        for i, h in enumerate(helper):
+            rid, pid = topo.addr(h, core)
+            full = topo.mask(core, h)
+            m = engines(full, count(full) // nf, i * (count(full) // nf))
+            tr.append(RemoteDMATransfer(dst_ids=[DstId(rid=rid, pnc=pid)], dma_engine_mask=m, remote_sem=S.qarr,
+                                        src=T.qs[:], dst=T.qs[:]))
+            left += count(m)
+        g.remote_dma_fused(tr, local_sem=S.sent)
+        m = topo.mask(core, direct[0])
+        for c in direct:
+            m &= topo.mask(core, c)
+        ids = [DstId(rid=topo.addr(c, core)[0], pnc=topo.addr(c, core)[1]) for c in direct]
+        g.remote_dma_fused([RemoteDMATransfer(dst_ids=ids, dma_engine_mask=m, remote_sem=S.qarr, srcs=[T.qs[:]],
+                                              dsts=[T.qs[:] for c in direct])], local_sem=S.sent)
+        left += count(m)
+        g.wait_ge(S.sent, left)
+        g.sync.wait_ge(S.sent, left)
+        g.sync.dma_start(T.ks[:], T.k[:, :]).then_inc(S.k, 16)
+        g.scalar.wait_ge(S.sent, left)
+        load_v(g.scalar)
+        o0 = W * own_slot
+        worker(g, T, [(S.q, 16)], [(S.k, 16)], [(S.v, 16), (S.vone, 1)], T.land[:, o0:o0 + 129], T.land[:, o0 + 129:o0 + 130])
+        back = count(topo.mask(direct[0], root))
+        acc1 = T.ps[:, 512 * 6:512 * 6 + 129]
+        merge(g, T, "m1", own_slot, 1 + len(direct), acc1, [(S.pk, 1), (S.retA, back * len(direct))], T.land[:, 129:130])
+        g.vector.wait_ge(S.m1a, 1)
+        g.vector.tensor_copy(T.land[:, 0:129], acc1).then_inc(S.m1done, 1)
+        n2 = 1 + nf
+        acc2 = T.ps[:, 512 * 7:512 * 7 + 129]
+        merge(g, T, "m2", 0, n2, acc2, [(S.m1done, 1), (S.retB, count(topo.mask(proxy[0], root)) * nf)], T.nM[:, 0:1])
+        dve = g.vector
+        dve.wait_ge(S.m2w, 1)
+        dve.tensor_tensor(T.wl[:, 0:n2], T.m2w[:, 0:n2], T.land[:, 128:W * (n2 - 1) + 129:W], AluOpType.mult).then_inc(S.wl, 1)
+        dve.wait_ge(S.wl, 1)
+        dve.tensor_reduce(T.L[:, 0:1], T.wl[:, 0:n2], X, AluOpType.add).then_inc(S.L, 1)
+        dve.wait_ge(S.L, 1)
+        dve.reciprocal(T.L[:, 1:2], T.L[:, 0:1]).then_inc(S.rL, 1)
+        dve.wait_ge(S.rL, 1)
+        dve.wait_ge(S.m2a, 1)
+        dve.tensor_scalar(T.ys[:], T.ps[:, 512 * 7:512 * 7 + 128], T.L[:, 1:2], None, AluOpType.mult).then_inc(S.ys, 1)
+        g.sync.wait_ge(S.ys, 1)
+        g.sync.dma_start(T.y[:, :], T.ys[:]).then_inc(S.y, 16)
+        g.sync.wait_ge(S.y, 16)
+        return
+
+    if core in helper:
+        p = proxy[helper.index(core)]
+        g.wait_ge(S.qarr, count(topo.mask(root, core)) // nf)
+        n = send(p, T.qs[:], T.qs[:], S.qarr, count(topo.mask(core, p)))
+        g.wait_ge(S.sent, n)
+        return
+
+    if core in far:
+        p = proxy[far.index(core)]
+        g.sync.dma_start(T.ks[:], T.k[:, :]).then_inc(S.k, 16)
+        load_v(g.scalar)
+        full = count(topo.mask(core, p))
+        g.wait_ge(S.k, 16)
+        n = send(p, T.ks[:], T.ks[:], S.karr, full)
+        g.wait_ge(S.v, 16)
+        g.wait_ge(S.vone, 1)
+        n += send(p, T.vs[:], T.vs[:], S.varr, full)
+        g.wait_ge(S.sent, n)
+        return
+
+    if core in direct or core in proxy:
+        if core in direct:
+            slot, ret = own_slot + 1 + direct.index(core), S.retA
+            g.sync.dma_start(T.ks[:], T.k[:, :]).then_inc(S.k, 16)
+            load_v(g.scalar)
+            q_ready = [(S.qarr, count(topo.mask(root, core)))]
+            k_ready, v_ready = [(S.k, 16)], [(S.v, 16), (S.vone, 1)]
+        else:
+            i = proxy.index(core)
+            slot, ret = 1 + i, S.retB
+            q_ready = [(S.qarr, count(topo.mask(helper[i], core)))]
+            k_ready = [(S.karr, count(topo.mask(far[i], core)))]
+            v_ready = [(S.varr, count(topo.mask(far[i], core)))]
+        constants(g, T)
+        worker(g, T, q_ready, k_ready, v_ready, T.pk[:, 0:129], T.pk[:, 129:130])
+        g.wait_ge(S.pk, 1)
+        n = send(root, T.land[:, W * slot:W * slot + PW], T.pk[:, 0:PW], ret, count(topo.mask(core, root)))
+        g.wait_ge(S.sent, n)

@@ -3,7 +3,7 @@ from concourse.mybir import AluOpType, AxisListType, ActivationFunctionType
 
 KB = 4
 W = 136
-PW = 130
+MW = 8
 NSLOT = 7
 
 SCRATCH = {
@@ -16,7 +16,9 @@ SCRATCH = {
     "dg": ("sbuf", [128, 128], "bfloat16"),
     "P": ("sbuf", [128, 512], "bfloat16"),
     "pk": ("sbuf", [128, W], "bfloat16"),
+    "pkm": ("sbuf", [128, MW], "bfloat16"),
     "land": ("sbuf", [128, NSLOT * W], "bfloat16"),
+    "mland": ("sbuf", [128, NSLOT * MW], "bfloat16"),
     "m1w": ("sbuf", [128, 4], "float32"),
     "m2w": ("sbuf", [128, 4], "float32"),
     "m1d": ("sbuf", [128, 512], "bfloat16"),
@@ -28,8 +30,8 @@ SCRATCH = {
     "ps": ("psum", [128, 8 * 512], "float32"),
 }
 SEMAPHORES = (["q", "k", "v", "vone", "ramp", "idn", "ones", "qarr", "karr", "varr", "sent", "st", "nm", "dg", "o", "pk",
-               "retA", "retB", "m1M", "m1w", "m1a", "m1done", "m2M", "m2w", "m2a", "wl", "L", "rL", "ys", "y"]
-              + ["sb%d" % b for b in range(KB)] + ["p%d" % b for b in range(KB)]
+               "mA", "mB", "m1M", "m1w", "m1a", "m1done", "m2M", "m2w", "m2a", "wl", "L", "rL", "ys", "y"]
+              + ["sb%d" % b for b in range(KB)] + ["p%d" % b for b in range(KB)] + ["ret%d" % j for j in range(NSLOT)]
               + ["m1d%d" % j for j in range(4)] + ["m2d%d" % j for j in range(4)])
 
 X = AxisListType.X
@@ -103,12 +105,12 @@ def worker(g, T, q_ready, k_ready, v_ready, pk_o, pk_m):
     dve.tensor_copy(pk_o, O).then_inc(S.pk, 1)
 
 
-def merge(g, T, pre, lo, n, acc, ready, negM):
+def merge(g, T, pre, lo, n, acc, m_ready, o_ready, negM):
     S, land = T.sem, T.land
     pe, dve, act = g.tensor, g.vector, g.scalar
-    negm = land[:, W * lo + 129:W * (lo + n - 1) + 130:W]
+    negm = T.mland[:, MW * lo:MW * (lo + n - 1) + 1:MW]
     w, d = T[pre + "w"], T[pre + "d"]
-    for s, v in ready:
+    for s, v in m_ready:
         dve.wait_ge(s, v)
     dve.tensor_reduce(negM, negm, X, AluOpType.min).then_inc(S[pre + "M"], 1)
     act.wait_ge(S[pre + "M"], 1)
@@ -117,6 +119,7 @@ def merge(g, T, pre, lo, n, acc, ready, negM):
     for j in range(n):
         act.activation(d[:, 128 * j:128 * j + 128], T.ident[:], ACT.Copy, scale=w[:, j:j + 1]).then_inc(S[pre + "d%d" % j], 1)
         pe.wait_ge(S[pre + "d%d" % j], 1)
+        pe.wait_ge(o_ready[j][0], o_ready[j][1])
         mm = pe.matmul(acc, d[:, 128 * j:128 * j + 128], land[:, W * (lo + j):W * (lo + j) + 129], j == 0, j == n - 1)
     mm.then_inc(S[pre + "a"], 1)
 
@@ -163,17 +166,22 @@ def rank_program(g, core, T, topo):
         g.scalar.wait_ge(S.sent, left)
         load_v(g.scalar)
         o0 = W * own_slot
-        worker(g, T, [(S.q, 16)], [(S.k, 16)], [(S.v, 16), (S.vone, 1)], T.land[:, o0:o0 + 129], T.land[:, o0 + 129:o0 + 130])
-        back = count(topo.mask(direct[0], root))
-        acc1 = T.ps[:, 512 * 6:512 * 6 + 129]
-        merge(g, T, "m1", own_slot, 1 + len(direct), acc1, [(S.pk, 1), (S.retA, back * len(direct))], T.land[:, 129:130])
-        g.vector.wait_ge(S.m1a, 1)
-        g.vector.tensor_copy(T.land[:, 0:129], acc1).then_inc(S.m1done, 1)
-        n2 = 1 + nf
-        acc2 = T.ps[:, 512 * 7:512 * 7 + 129]
-        merge(g, T, "m2", 0, n2, acc2, [(S.m1done, 1), (S.retB, count(topo.mask(proxy[0], root)) * nf)], T.nM[:, 0:1])
+        worker(g, T, [(S.q, 16)], [(S.k, 16)], [(S.v, 16), (S.vone, 1)], T.land[:, o0:o0 + 129],
+               T.mland[:, MW * own_slot:MW * own_slot + 1])
         dve = g.vector
-        dve.wait_ge(S.m2w, 1)
+        backs = [count(topo.mask(c, root)) for c in direct]
+        acc1 = T.ps[:, 512 * 6:512 * 6 + 129]
+        merge(g, T, "m1", own_slot, 1 + len(direct), acc1, [(S.nm, 1), (S.mA, sum(backs))],
+              [(S.pk, 1)] + [(S["ret%d" % (own_slot + 1 + i)], backs[i]) for i in range(len(direct))], T.mland[:, 0:1])
+        dve.wait_ge(S.m1a, 1)
+        dve.tensor_copy(T.land[:, 0:129], acc1).then_inc(S.m1done, 1)
+        n2 = 1 + nf
+        backs = [count(topo.mask(p, root)) for p in proxy]
+        landed = [(S["ret%d" % (1 + i)], backs[i]) for i in range(nf)]
+        acc2 = T.ps[:, 512 * 7:512 * 7 + 129]
+        merge(g, T, "m2", 0, n2, acc2, [(S.m1M, 1), (S.mB, sum(backs))], [(S.m1done, 1)] + landed, T.nM[:, 0:1])
+        for s, v in [(S.m2w, 1), (S.m1done, 1)] + landed:
+            dve.wait_ge(s, v)
         dve.tensor_tensor(T.wl[:, 0:n2], T.m2w[:, 0:n2], T.land[:, 128:W * (n2 - 1) + 129:W], AluOpType.mult).then_inc(S.wl, 1)
         dve.wait_ge(S.wl, 1)
         dve.tensor_reduce(T.L[:, 0:1], T.wl[:, 0:n2], X, AluOpType.add).then_inc(S.L, 1)
@@ -209,19 +217,22 @@ def rank_program(g, core, T, topo):
 
     if core in direct or core in proxy:
         if core in direct:
-            slot, ret = own_slot + 1 + direct.index(core), S.retA
+            slot, msem = own_slot + 1 + direct.index(core), S.mA
             g.sync.dma_start(T.ks[:], T.k[:, :]).then_inc(S.k, 16)
             load_v(g.scalar)
             q_ready = [(S.qarr, count(topo.mask(root, core)))]
             k_ready, v_ready = [(S.k, 16)], [(S.v, 16), (S.vone, 1)]
         else:
             i = proxy.index(core)
-            slot, ret = 1 + i, S.retB
+            slot, msem = 1 + i, S.mB
             q_ready = [(S.qarr, count(topo.mask(helper[i], core)))]
             k_ready = [(S.karr, count(topo.mask(far[i], core)))]
             v_ready = [(S.varr, count(topo.mask(far[i], core)))]
         constants(g, T)
-        worker(g, T, q_ready, k_ready, v_ready, T.pk[:, 0:129], T.pk[:, 129:130])
+        worker(g, T, q_ready, k_ready, v_ready, T.pk[:, 0:129], T.pkm[:, 0:1])
+        full = count(topo.mask(core, root))
+        g.wait_ge(S.nm, 1)
+        n = send(root, T.mland[:, MW * slot:MW * slot + 1], T.pkm[:, 0:1], msem, full)
         g.wait_ge(S.pk, 1)
-        n = send(root, T.land[:, W * slot:W * slot + PW], T.pk[:, 0:PW], ret, count(topo.mask(core, root)))
+        n += send(root, T.land[:, W * slot:W * slot + 129], T.pk[:, 0:129], S["ret%d" % slot], full)
         g.wait_ge(S.sent, n)

@@ -4,12 +4,18 @@ from concourse.mybir import AluOpType, AxisListType, ActivationFunctionType
 KB = 4
 W = 136
 MW = 8
-NSLOT = 7
+NI = 6
+CUTS = [0, 32, 64, 96, 112, 128]
 
 SCRATCH = {
+    "qd": ("dram", [128, 128], "bfloat16"),
     "qs": ("sbuf", [128, 128], "bfloat16"),
     "ks": ("sbuf", [128, 512], "bfloat16"),
+    "kd": ("dram", [128, 512], "bfloat16"),
+    "vd": ("dram", [128, 512], "bfloat16"),
+    "vr": ("sbuf", [128, 512], "bfloat16"),
     "vs": ("sbuf", [128, KB, W], "bfloat16"),
+    "wrm": ("sbuf", [128, 8], "float32"),
     "ramp": ("sbuf", [128, 128], "float32"),
     "ident": ("sbuf", [128, 128], "bfloat16"),
     "ones": ("sbuf", [128, 128], "bfloat16"),
@@ -17,22 +23,19 @@ SCRATCH = {
     "P": ("sbuf", [128, 512], "bfloat16"),
     "pk": ("sbuf", [128, W], "bfloat16"),
     "pkm": ("sbuf", [128, MW], "bfloat16"),
-    "land": ("sbuf", [128, NSLOT * W], "bfloat16"),
-    "mland": ("sbuf", [128, NSLOT * MW], "bfloat16"),
-    "m1w": ("sbuf", [128, 4], "float32"),
-    "m2w": ("sbuf", [128, 4], "float32"),
-    "m1d": ("sbuf", [128, 512], "bfloat16"),
-    "m2d": ("sbuf", [128, 512], "bfloat16"),
+    "land": ("sbuf", [128, NI * W], "bfloat16"),
+    "mland": ("sbuf", [128, NI * MW], "bfloat16"),
+    "w": ("sbuf", [128, 8], "float32"),
+    "d": ("sbuf", [128, NI * 128], "bfloat16"),
     "nM": ("sbuf", [128, 8], "bfloat16"),
-    "wl": ("sbuf", [128, 4], "float32"),
     "L": ("sbuf", [128, 4], "float32"),
     "ys": ("sbuf", [128, 128], "bfloat16"),
     "ps": ("psum", [128, 8 * 512], "float32"),
 }
-SEMAPHORES = (["q", "k", "v", "vone", "ramp", "idn", "ones", "qarr", "karr", "varr", "sent", "st", "nm", "dg", "o", "pk",
-               "mA", "mB", "m1M", "m1w", "m1a", "m1done", "m2M", "m2w", "m2a", "wl", "L", "rL", "ys", "y"]
-              + ["sb%d" % b for b in range(KB)] + ["p%d" % b for b in range(KB)] + ["ret%d" % j for j in range(NSLOT)]
-              + ["m1d%d" % j for j in range(4)] + ["m2d%d" % j for j in range(4)])
+SEMAPHORES = (["qd", "q", "k", "v", "vone", "ramp", "idn", "ones", "qarr", "karr", "varr", "sent", "st", "nm", "dg", "o", "pk",
+               "mA", "M", "w", "acc", "rL", "ys", "y"]
+              + ["sb%d" % b for b in range(KB)] + ["p%d" % b for b in range(KB)] + ["ret%d" % j for j in range(NI)]
+              + ["d%d" % j for j in range(NI)])
 
 X = AxisListType.X
 ACT = ActivationFunctionType
@@ -64,16 +67,26 @@ def plan(T, topo):
     return root, direct, far, proxy, helper
 
 
-def constants(g, T):
+def identity(g, T):
     S = T.sem
     g.iota(T.ramp[:], [[-1, 128]], 0, 1, allow_small_or_imprecise_dtypes=True).then_inc(S.ramp, 1)
     g.vector.wait_ge(S.ramp, 1)
     g.vector.tensor_scalar(T.ident[:], T.ramp[:], 0.0, None, AluOpType.is_equal).then_inc(S.idn, 1)
+
+
+def constants(g, T):
+    S = T.sem
+    identity(g, T)
     g.scalar.wait_ge(S.ramp, 1)
     g.scalar.activation(T.ones[:], T.ramp[:], ACT.Exp, scale=0.0).then_inc(S.ones, 1)
 
 
-def worker(g, T, q_ready, k_ready, v_ready, pk_o, pk_m):
+def exp_table(g, T, src, sem, n):
+    g.scalar.wait_ge(sem, n)
+    g.scalar.activation(T.wrm[:, 0:8], src[:, 0:8], ACT.Exp, scale=0.0)
+
+
+def worker(g, T, q_ready, k_ready, v_ready, pk_o, pk_m, idn_n=1, ones_n=1, v_fix=None):
     S, ps = T.sem, T.ps
     pe, dve, act = g.tensor, g.vector, g.scalar
     ST = ps[:, 0:512]
@@ -87,10 +100,12 @@ def worker(g, T, q_ready, k_ready, v_ready, pk_o, pk_m):
     dve.wait_ge(S.st, 1)
     dve.tensor_reduce(pk_m, ST, X, AluOpType.max, negate=True).then_inc(S.nm, 1)
     dve.wait_ge(S.nm, 1)
-    dve.wait_ge(S.idn, 1)
+    dve.wait_ge(S.idn, idn_n)
     dve.tensor_scalar(T.dg[:], T.ident[:], pk_m, None, AluOpType.mult).then_inc(S.dg, 1)
+    if v_fix is not None:
+        v_fix()
     pe.wait_ge(S.dg, 1)
-    pe.wait_ge(S.ones, 1)
+    pe.wait_ge(S.ones, ones_n)
     for b in range(KB):
         pe.matmul(SB[b], T.ones[:], T.dg[:], False, True).then_inc(S["sb%d" % b], 1)
         act.wait_ge(S["sb%d" % b], 1)
@@ -105,30 +120,35 @@ def worker(g, T, q_ready, k_ready, v_ready, pk_o, pk_m):
     dve.tensor_copy(pk_o, O).then_inc(S.pk, 1)
 
 
-def merge(g, T, pre, lo, n, acc, m_ready, o_ready, negM):
-    S, land = T.sem, T.land
+def merge(g, T, acc, m_ready, o_ready):
+    S, land, w, d = T.sem, T.land, T.w, T.d
     pe, dve, act = g.tensor, g.vector, g.scalar
-    negm = T.mland[:, MW * lo:MW * (lo + n - 1) + 1:MW]
-    w, d = T[pre + "w"], T[pre + "d"]
+    n = len(o_ready)
+    negm = T.mland[:, 0:MW * (n - 1) + 1:MW]
+    negM = T.nM[:, 0:1]
     for s, v in m_ready:
         dve.wait_ge(s, v)
-    dve.tensor_reduce(negM, negm, X, AluOpType.min).then_inc(S[pre + "M"], 1)
-    act.wait_ge(S[pre + "M"], 1)
-    act.activation(w[:, 0:n], negm, ACT.Exp, bias=negM, scale=-1.0).then_inc(S[pre + "w"], 1)
-    act.wait_ge(S[pre + "w"], 1)
+    dve.tensor_reduce(negM, negm, X, AluOpType.min).then_inc(S.M, 1)
+    act.wait_ge(S.M, 1)
+    act.activation(w[:, 0:n], negm, ACT.Exp, bias=negM, scale=-1.0).then_inc(S.w, 1)
+    act.wait_ge(S.w, 1)
+    dve.wait_ge(S.w, 1)
     for j in range(n):
-        act.activation(d[:, 128 * j:128 * j + 128], T.ident[:], ACT.Copy, scale=w[:, j:j + 1]).then_inc(S[pre + "d%d" % j], 1)
-        pe.wait_ge(S[pre + "d%d" % j], 1)
+        dj = d[:, 128 * j:128 * j + 128]
+        if j % 2 == 0:
+            dve.tensor_scalar(dj, T.ident[:], w[:, j:j + 1], None, AluOpType.mult).then_inc(S["d%d" % j], 1)
+        else:
+            act.activation(dj, T.ident[:], ACT.Copy, scale=w[:, j:j + 1]).then_inc(S["d%d" % j], 1)
+        pe.wait_ge(S["d%d" % j], 1)
         pe.wait_ge(o_ready[j][0], o_ready[j][1])
-        mm = pe.matmul(acc, d[:, 128 * j:128 * j + 128], land[:, W * (lo + j):W * (lo + j) + 129], j == 0, j == n - 1)
-    mm.then_inc(S[pre + "a"], 1)
+        mm = pe.matmul(acc, dj, land[:, W * j:W * j + 129], j == 0, j == n - 1)
+    mm.then_inc(S.acc, 1)
 
 
 def rank_program(g, core, T, topo):
     S = T.sem
     root, direct, far, proxy, helper = plan(T, topo)
-    nf = len(far)
-    own_slot = 1 + nf
+    items = [root, direct[0]] + proxy + direct[1:]
 
     def send(dst, out, in_, sem, n, skip=0):
         rid, pid = topo.addr(dst, core)
@@ -136,60 +156,59 @@ def rank_program(g, core, T, topo):
         g.remote_dma(out_ap=out, in_ap=in_, remote_sem=sem, local_sem=S.sent, pid=pid, routing_id=rid, dma_engine_mask=m)
         return count(m)
 
-    def load_v(queue):
+    def v_ones():
         g.vector.memset(T.vs[:, :, 128:W], 1.0).then_inc(S.vone, 1)
-        queue.dma_start(T.vs[:, :, 0:128], T.v[:, :]).then_inc(S.v, 16)
+
+    def v_load(queue):
+        queue.dma_start(T.vr[:, :], T.v[:, :]).then_inc(S.v, 16)
+
+    def v_fix(sem=S.v, n=16):
+        g.vector.wait_ge(sem, n)
+        for b in range(KB):
+            g.vector.tensor_copy(T.vs[:, b, 0:128], T.vr[:, 128 * b:128 * b + 128]).then_inc(S.vone, 1)
+
+    v_done = [(S.vone, 1 + KB)]
+
+    off = topo.mask(root, direct[0])
+    for c in direct:
+        off &= topo.mask(root, c)
+    on = topo.mask(root, helper[0])
+    for h in helper:
+        on &= topo.mask(root, h)
+    on &= ~off
 
     if core == root:
+        g.sync.dma_start(T.qd[:, :], T.q[:, :]).then_inc(S.qd, 16)
         g.sync.dma_start(T.qs[:], T.q[:, :]).then_inc(S.q, 16)
-        constants(g, T)
-        g.wait_ge(S.q, 16)
-        tr, left = [], 0
-        for i, h in enumerate(helper):
-            rid, pid = topo.addr(h, core)
-            full = topo.mask(core, h)
-            m = engines(full, count(full) // nf, i * (count(full) // nf))
-            tr.append(RemoteDMATransfer(dst_ids=[DstId(rid=rid, pnc=pid)], dma_engine_mask=m, remote_sem=S.qarr,
-                                        src=T.qs[:], dst=T.qs[:]))
-            left += count(m)
-        g.remote_dma_fused(tr, local_sem=S.sent)
-        m = topo.mask(core, direct[0])
-        for c in direct:
-            m &= topo.mask(core, c)
+        g.sync.dma_start(T.ks[:], T.k[:, :]).then_inc(S.k, 16)
+        g.vector.memset(T.ones[:], 1.0).then_inc(S.ones, 1)
+        g.wait_ge(S.ones, 1)
+        left = send(direct[0], T.ones[:], T.ones[:], S.ones, count(off))
+        exp_table(g, T, T.ones, S.ones, 1)
+        v_ones()
+        g.wait_ge(S.qd, 16)
         ids = [DstId(rid=topo.addr(c, core)[0], pnc=topo.addr(c, core)[1]) for c in direct]
-        g.remote_dma_fused([RemoteDMATransfer(dst_ids=ids, dma_engine_mask=m, remote_sem=S.qarr, srcs=[T.qs[:]],
-                                              dsts=[T.qs[:] for c in direct])], local_sem=S.sent)
-        left += count(m)
+        hids = [DstId(rid=topo.addr(h, core)[0], pnc=topo.addr(h, core)[1]) for h in helper]
+        g.remote_dma_fused([
+            RemoteDMATransfer(dst_ids=hids, dma_engine_mask=on, remote_sem=S.qarr, srcs=[T.qd[:, :]],
+                              dsts=[T.qd[:, :] for h in helper]),
+            RemoteDMATransfer(dst_ids=ids, dma_engine_mask=off, remote_sem=S.qarr, srcs=[T.qd[:, :]],
+                              dsts=[T.qs[:] for c in direct])], local_sem=S.sent)
+        left += count(on) + count(off)
         g.wait_ge(S.sent, left)
         g.sync.wait_ge(S.sent, left)
-        g.sync.dma_start(T.ks[:], T.k[:, :]).then_inc(S.k, 16)
-        g.scalar.wait_ge(S.sent, left)
-        load_v(g.scalar)
-        o0 = W * own_slot
-        worker(g, T, [(S.q, 16)], [(S.k, 16)], [(S.v, 16), (S.vone, 1)], T.land[:, o0:o0 + 129],
-               T.mland[:, MW * own_slot:MW * own_slot + 1])
+        v_load(g.sync)
+        backs = [count(topo.mask(c, root)) for c in items[1:]]
+        worker(g, T, [(S.q, 16)], [(S.k, 16)], v_done, T.land[:, 0:129], T.mland[:, 0:1], idn_n=sum(backs), v_fix=v_fix)
         dve = g.vector
-        backs = [count(topo.mask(c, root)) for c in direct]
-        acc1 = T.ps[:, 512 * 6:512 * 6 + 129]
-        merge(g, T, "m1", own_slot, 1 + len(direct), acc1, [(S.nm, 1), (S.mA, sum(backs))],
-              [(S.pk, 1)] + [(S["ret%d" % (own_slot + 1 + i)], backs[i]) for i in range(len(direct))], T.mland[:, 0:1])
-        dve.wait_ge(S.m1a, 1)
-        dve.tensor_copy(T.land[:, 0:129], acc1).then_inc(S.m1done, 1)
-        n2 = 1 + nf
-        backs = [count(topo.mask(p, root)) for p in proxy]
-        landed = [(S["ret%d" % (1 + i)], backs[i]) for i in range(nf)]
-        acc2 = T.ps[:, 512 * 7:512 * 7 + 129]
-        merge(g, T, "m2", 0, n2, acc2, [(S.m1M, 1), (S.mB, sum(backs))], [(S.m1done, 1)] + landed, T.nM[:, 0:1])
-        for s, v in [(S.m2w, 1), (S.m1done, 1)] + landed:
-            dve.wait_ge(s, v)
-        dve.tensor_tensor(T.wl[:, 0:n2], T.m2w[:, 0:n2], T.land[:, 128:W * (n2 - 1) + 129:W], AluOpType.mult).then_inc(S.wl, 1)
-        dve.wait_ge(S.wl, 1)
-        dve.tensor_reduce(T.L[:, 0:1], T.wl[:, 0:n2], X, AluOpType.add).then_inc(S.L, 1)
-        dve.wait_ge(S.L, 1)
-        dve.reciprocal(T.L[:, 1:2], T.L[:, 0:1]).then_inc(S.rL, 1)
+        acc = T.ps[:, 512 * 6:512 * 6 + 129]
+        g.scalar.wait_ge(S.idn, sum(backs))
+        merge(g, T, acc, [(S.nm, 1), (S.mA, sum(backs))],
+              [(S.pk, 1)] + [(S["ret%d" % (1 + i)], backs[i]) for i in range(len(backs))])
+        dve.wait_ge(S.acc, 1)
+        dve.reciprocal(T.L[:, 0:1], T.ps[:, 512 * 6 + 128:512 * 6 + 129]).then_inc(S.rL, 1)
         dve.wait_ge(S.rL, 1)
-        dve.wait_ge(S.m2a, 1)
-        dve.tensor_scalar(T.ys[:], T.ps[:, 512 * 7:512 * 7 + 128], T.L[:, 1:2], None, AluOpType.mult).then_inc(S.ys, 1)
+        dve.tensor_scalar(T.ys[:], T.ps[:, 512 * 6:512 * 6 + 128], T.L[:, 0:1], None, AluOpType.mult).then_inc(S.ys, 1)
         g.sync.wait_ge(S.ys, 1)
         g.sync.dma_start(T.y[:, :], T.ys[:]).then_inc(S.y, 16)
         g.sync.wait_ge(S.y, 16)
@@ -197,42 +216,65 @@ def rank_program(g, core, T, topo):
 
     if core in helper:
         p = proxy[helper.index(core)]
-        g.wait_ge(S.qarr, count(topo.mask(root, core)) // nf)
-        n = send(p, T.qs[:], T.qs[:], S.qarr, count(topo.mask(core, p)))
+        full = count(topo.mask(core, p))
+        identity(g, T)
+        g.wait_ge(S.idn, 1)
+        n = send(p, T.ident[:], T.ident[:], S.idn, full)
+        g.wait_ge(S.qarr, count(on))
+        n += send(p, T.qs[:], T.qd[:, :], S.qarr, full)
         g.wait_ge(S.sent, n)
         return
 
     if core in far:
         p = proxy[far.index(core)]
-        g.sync.dma_start(T.ks[:], T.k[:, :]).then_inc(S.k, 16)
-        load_v(g.scalar)
+        g.sync.dma_start(T.kd[:, :], T.k[:, :]).then_inc(S.k, 16)
+        g.sync.dma_start(T.vd[:, :], T.v[:, :]).then_inc(S.v, 16)
+        g.vector.memset(T.ones[:], 1.0).then_inc(S.ones, 1)
         full = count(topo.mask(core, p))
+        g.wait_ge(S.ones, 1)
+        n = send(p, T.ones[:], T.ones[:], S.ones, full)
         g.wait_ge(S.k, 16)
-        n = send(p, T.ks[:], T.ks[:], S.karr, full)
+        n += send(p, T.ks[:], T.kd[:, :], S.karr, full)
         g.wait_ge(S.v, 16)
-        g.wait_ge(S.vone, 1)
-        n += send(p, T.vs[:], T.vs[:], S.varr, full)
+        n += send(p, T.vr[:, :], T.vd[:, :], S.varr, full)
         g.wait_ge(S.sent, n)
         return
 
     if core in direct or core in proxy:
+        slot = items.index(core)
+        late_v = None
         if core in direct:
-            slot, msem = own_slot + 1 + direct.index(core), S.mA
             g.sync.dma_start(T.ks[:], T.k[:, :]).then_inc(S.k, 16)
-            load_v(g.scalar)
-            q_ready = [(S.qarr, count(topo.mask(root, core)))]
-            k_ready, v_ready = [(S.k, 16)], [(S.v, 16), (S.vone, 1)]
+            v_load(g.scalar)
+            idn_n = ones_n = 1
+            if core == direct[0]:
+                ones_n = count(off)
+                identity(g, T)
+                exp_table(g, T, T.ramp, S.ramp, 1)
+            else:
+                constants(g, T)
+            v_ones()
+            v_fix()
+            q_ready = [(S.qarr, count(off))]
+            k_ready = [(S.k, 16)]
         else:
             i = proxy.index(core)
-            slot, msem = 1 + i, S.mB
+            fed = count(topo.mask(far[i], core))
             q_ready = [(S.qarr, count(topo.mask(helper[i], core)))]
-            k_ready = [(S.karr, count(topo.mask(far[i], core)))]
-            v_ready = [(S.varr, count(topo.mask(far[i], core)))]
-        constants(g, T)
-        worker(g, T, q_ready, k_ready, v_ready, T.pk[:, 0:129], T.pkm[:, 0:1])
+            k_ready = [(S.karr, fed)]
+            idn_n, ones_n = count(topo.mask(helper[i], core)), fed
+            exp_table(g, T, T.ones, S.ones, ones_n)
+            v_ones()
+
+            def late_v():
+                v_fix(S.varr, fed)
+        worker(g, T, q_ready, k_ready, v_done, T.pk[:, 0:129], T.pkm[:, 0:1], idn_n, ones_n, late_v)
         full = count(topo.mask(core, root))
+        c0, c1 = CUTS[slot - 1], CUTS[slot]
+        g.wait_ge(S.idn, idn_n)
+        n = send(root, T.ident[:, c0:c1], T.ident[:, c0:c1], S.idn, full)
         g.wait_ge(S.nm, 1)
-        n = send(root, T.mland[:, MW * slot:MW * slot + 1], T.pkm[:, 0:1], msem, full)
+        n += send(root, T.mland[:, MW * slot:MW * slot + 1], T.pkm[:, 0:1], S.mA, full)
         g.wait_ge(S.pk, 1)
         n += send(root, T.land[:, W * slot:W * slot + 129], T.pk[:, 0:129], S["ret%d" % slot], full)
         g.wait_ge(S.sent, n)

from concourse.bass import DstId, RemoteDMATransfer
from concourse.mybir import AluOpType, AxisListType, ActivationFunctionType

KB = 4
W = 136
MW = 8
NI = 6
CUTS = [0, 32, 64, 96, 112, 128]

SCRATCH = {
    "qd": ("dram", [128, 128], "bfloat16"),
    "qs": ("sbuf", [128, 128], "bfloat16"),
    "ks": ("sbuf", [128, 512], "bfloat16"),
    "kd": ("dram", [128, 512], "bfloat16"),
    "vd": ("dram", [128, 512], "bfloat16"),
    "vr": ("sbuf", [128, 512], "bfloat16"),
    "vs": ("sbuf", [128, KB, W], "bfloat16"),
    "wrm": ("sbuf", [128, 8], "float32"),
    "ramp": ("sbuf", [128, 128], "float32"),
    "ident": ("sbuf", [128, 128], "bfloat16"),
    "ones": ("sbuf", [128, 128], "bfloat16"),
    "dg": ("sbuf", [128, 128], "bfloat16"),
    "P": ("sbuf", [128, 512], "bfloat16"),
    "pk": ("sbuf", [128, W], "bfloat16"),
    "pkm": ("sbuf", [128, MW], "bfloat16"),
    "land": ("sbuf", [128, NI * W], "bfloat16"),
    "mland": ("sbuf", [128, NI * MW], "bfloat16"),
    "w": ("sbuf", [128, 8], "float32"),
    "d": ("sbuf", [128, NI * 128], "bfloat16"),
    "nM": ("sbuf", [128, 8], "bfloat16"),
    "L": ("sbuf", [128, 4], "float32"),
    "ys": ("sbuf", [128, 128], "bfloat16"),
    "ps": ("psum", [128, 8 * 512], "float32"),
}
SEMAPHORES = (["qd", "q", "k", "v", "vone", "ramp", "idn", "ones", "qarr", "karr", "varr", "sent", "st", "nm", "dg", "o", "pk",
               "mA", "M", "w", "acc", "rL", "ys", "y"]
              + ["sb%d" % b for b in range(KB)] + ["p%d" % b for b in range(KB)] + ["ret%d" % j for j in range(NI)]
              + ["d%d" % j for j in range(NI)])

X = AxisListType.X
ACT = ActivationFunctionType


def engines(mask, n, skip=0):
    bits = [i for i in range(mask.bit_length()) if (mask >> i) & 1][skip:skip + n]
    return sum(1 << i for i in bits)


def count(mask):
    return bin(mask).count("1")


def plan(T, topo):
    root = T.cores[T.root]
    world = (max(topo.host(c) for c in T.cores) + 1) * topo.CORES_PER_HOST

    def neighbours(c):
        return [x for x in range(world) if x not in T.cores and topo.host(x) == topo.host(c)
                and topo.chip(x) == topo.chip(c) and topo.die(x) == topo.die(c)]

    direct = [c for c in T.cores if c != root and topo.may_write(root, c) and topo.may_write(c, root)]
    far = [c for c in T.cores if c != root and c not in direct]
    proxy = [[x for x in neighbours(c) if topo.may_write(x, root)][0] for c in far]
    helper = []
    for p in proxy:
        helper.append([x for x in neighbours(root) if topo.may_write(x, p) and x not in helper][0])
    return root, direct, far, proxy, helper


def identity(g, T):
    S = T.sem
    g.iota(T.ramp[:], [[-1, 128]], 0, 1, allow_small_or_imprecise_dtypes=True).then_inc(S.ramp, 1)
    g.vector.wait_ge(S.ramp, 1)
    g.vector.tensor_scalar(T.ident[:], T.ramp[:], 0.0, None, AluOpType.is_equal).then_inc(S.idn, 1)


def constants(g, T):
    S = T.sem
    identity(g, T)
    g.scalar.wait_ge(S.ramp, 1)
    g.scalar.activation(T.ones[:], T.ramp[:], ACT.Exp, scale=0.0).then_inc(S.ones, 1)


def exp_table(g, T, src, sem, n):
    g.scalar.wait_ge(sem, n)
    g.scalar.activation(T.wrm[:, 0:8], src[:, 0:8], ACT.Exp, scale=0.0)


def worker(g, T, q_ready, k_ready, v_ready, pk_o, pk_m, idn_n=1, ones_n=1, v_fix=None):
    S, ps = T.sem, T.ps
    pe, dve, act = g.tensor, g.vector, g.scalar
    ST = ps[:, 0:512]
    SB = [ps[:, 512 * (1 + b):512 * (1 + b) + 128] for b in range(KB)]
    O = ps[:, 512 * 5:512 * 5 + 129]
    for s, n in q_ready + k_ready:
        pe.wait_ge(s, n)
    pe.matmul(ST, T.qs[:], T.ks[:], True, True).then_inc(S.st, 1)
    for b in range(KB):
        pe.matmul(SB[b], T.ks[:, 128 * b:128 * b + 128], T.qs[:], True, False)
    dve.wait_ge(S.st, 1)
    dve.tensor_reduce(pk_m, ST, X, AluOpType.max, negate=True).then_inc(S.nm, 1)
    dve.wait_ge(S.nm, 1)
    dve.wait_ge(S.idn, idn_n)
    dve.tensor_scalar(T.dg[:], T.ident[:], pk_m, None, AluOpType.mult).then_inc(S.dg, 1)
    if v_fix is not None:
        v_fix()
    pe.wait_ge(S.dg, 1)
    pe.wait_ge(S.ones, ones_n)
    for b in range(KB):
        pe.matmul(SB[b], T.ones[:], T.dg[:], False, True).then_inc(S["sb%d" % b], 1)
        act.wait_ge(S["sb%d" % b], 1)
        act.activation(T.P[:, 128 * b:128 * b + 128], SB[b], ACT.Exp).then_inc(S["p%d" % b], 1)
    for s, n in v_ready:
        pe.wait_ge(s, n)
    for b in range(KB):
        pe.wait_ge(S["p%d" % b], 1)
        mm = pe.matmul(O, T.P[:, 128 * b:128 * b + 128], T.vs[:, b, 0:129], b == 0, b == KB - 1)
    mm.then_inc(S.o, 1)
    dve.wait_ge(S.o, 1)
    dve.tensor_copy(pk_o, O).then_inc(S.pk, 1)


def merge(g, T, acc, m_ready, o_ready):
    S, land, w, d = T.sem, T.land, T.w, T.d
    pe, dve, act = g.tensor, g.vector, g.scalar
    n = len(o_ready)
    negm = T.mland[:, 0:MW * (n - 1) + 1:MW]
    negM = T.nM[:, 0:1]
    for s, v in m_ready:
        dve.wait_ge(s, v)
    dve.tensor_reduce(negM, negm, X, AluOpType.min).then_inc(S.M, 1)
    act.wait_ge(S.M, 1)
    act.activation(w[:, 0:n], negm, ACT.Exp, bias=negM, scale=-1.0).then_inc(S.w, 1)
    act.wait_ge(S.w, 1)
    dve.wait_ge(S.w, 1)
    for j in range(n):
        dj = d[:, 128 * j:128 * j + 128]
        if j % 2 == 0:
            dve.tensor_scalar(dj, T.ident[:], w[:, j:j + 1], None, AluOpType.mult).then_inc(S["d%d" % j], 1)
        else:
            act.activation(dj, T.ident[:], ACT.Copy, scale=w[:, j:j + 1]).then_inc(S["d%d" % j], 1)
        pe.wait_ge(S["d%d" % j], 1)
        pe.wait_ge(o_ready[j][0], o_ready[j][1])
        mm = pe.matmul(acc, dj, land[:, W * j:W * j + 129], j == 0, j == n - 1)
    mm.then_inc(S.acc, 1)


def rank_program(g, core, T, topo):
    S = T.sem
    root, direct, far, proxy, helper = plan(T, topo)
    items = [root, direct[0]] + proxy + direct[1:]

    def send(dst, out, in_, sem, n, skip=0):
        rid, pid = topo.addr(dst, core)
        m = engines(topo.mask(core, dst), n, skip)
        g.remote_dma(out_ap=out, in_ap=in_, remote_sem=sem, local_sem=S.sent, pid=pid, routing_id=rid, dma_engine_mask=m)
        return count(m)

    def v_ones():
        g.vector.memset(T.vs[:, :, 128:W], 1.0).then_inc(S.vone, 1)

    def v_load(queue):
        queue.dma_start(T.vr[:, :], T.v[:, :]).then_inc(S.v, 16)

    def v_fix(sem=S.v, n=16):
        g.vector.wait_ge(sem, n)
        for b in range(KB):
            g.vector.tensor_copy(T.vs[:, b, 0:128], T.vr[:, 128 * b:128 * b + 128]).then_inc(S.vone, 1)

    v_done = [(S.vone, 1 + KB)]

    off = topo.mask(root, direct[0])
    for c in direct:
        off &= topo.mask(root, c)
    on = topo.mask(root, helper[0])
    for h in helper:
        on &= topo.mask(root, h)
    on &= ~off

    if core == root:
        g.sync.dma_start(T.qd[:, :], T.q[:, :]).then_inc(S.qd, 16)
        g.sync.dma_start(T.qs[:], T.q[:, :]).then_inc(S.q, 16)
        g.sync.dma_start(T.ks[:], T.k[:, :]).then_inc(S.k, 16)
        g.vector.memset(T.ones[:], 1.0).then_inc(S.ones, 1)
        g.wait_ge(S.ones, 1)
        left = send(direct[0], T.ones[:], T.ones[:], S.ones, count(off))
        exp_table(g, T, T.ones, S.ones, 1)
        v_ones()
        g.wait_ge(S.qd, 16)
        ids = [DstId(rid=topo.addr(c, core)[0], pnc=topo.addr(c, core)[1]) for c in direct]
        hids = [DstId(rid=topo.addr(h, core)[0], pnc=topo.addr(h, core)[1]) for h in helper]
        g.remote_dma_fused([
            RemoteDMATransfer(dst_ids=hids, dma_engine_mask=on, remote_sem=S.qarr, srcs=[T.qd[:, :]],
                              dsts=[T.qd[:, :] for h in helper]),
            RemoteDMATransfer(dst_ids=ids, dma_engine_mask=off, remote_sem=S.qarr, srcs=[T.qd[:, :]],
                              dsts=[T.qs[:] for c in direct])], local_sem=S.sent)
        left += count(on) + count(off)
        g.wait_ge(S.sent, left)
        g.sync.wait_ge(S.sent, left)
        v_load(g.sync)
        backs = [count(topo.mask(c, root)) for c in items[1:]]
        worker(g, T, [(S.q, 16)], [(S.k, 16)], v_done, T.land[:, 0:129], T.mland[:, 0:1], idn_n=sum(backs), v_fix=v_fix)
        dve = g.vector
        acc = T.ps[:, 512 * 6:512 * 6 + 129]
        g.scalar.wait_ge(S.idn, sum(backs))
        merge(g, T, acc, [(S.nm, 1), (S.mA, sum(backs))],
              [(S.pk, 1)] + [(S["ret%d" % (1 + i)], backs[i]) for i in range(len(backs))])
        dve.wait_ge(S.acc, 1)
        dve.reciprocal(T.L[:, 0:1], T.ps[:, 512 * 6 + 128:512 * 6 + 129]).then_inc(S.rL, 1)
        dve.wait_ge(S.rL, 1)
        dve.tensor_scalar(T.ys[:], T.ps[:, 512 * 6:512 * 6 + 128], T.L[:, 0:1], None, AluOpType.mult).then_inc(S.ys, 1)
        g.sync.wait_ge(S.ys, 1)
        g.sync.dma_start(T.y[:, :], T.ys[:]).then_inc(S.y, 16)
        g.sync.wait_ge(S.y, 16)
        return

    if core in helper:
        p = proxy[helper.index(core)]
        full = count(topo.mask(core, p))
        identity(g, T)
        g.wait_ge(S.idn, 1)
        n = send(p, T.ident[:], T.ident[:], S.idn, full)
        g.wait_ge(S.qarr, count(on))
        n += send(p, T.qs[:], T.qd[:, :], S.qarr, full)
        g.wait_ge(S.sent, n)
        return

    if core in far:
        p = proxy[far.index(core)]
        g.sync.dma_start(T.kd[:, :], T.k[:, :]).then_inc(S.k, 16)
        g.sync.dma_start(T.vd[:, :], T.v[:, :]).then_inc(S.v, 16)
        g.vector.memset(T.ones[:], 1.0).then_inc(S.ones, 1)
        full = count(topo.mask(core, p))
        g.wait_ge(S.ones, 1)
        n = send(p, T.ones[:], T.ones[:], S.ones, full)
        g.wait_ge(S.k, 16)
        n += send(p, T.ks[:], T.kd[:, :], S.karr, full)
        g.wait_ge(S.v, 16)
        n += send(p, T.vr[:, :], T.vd[:, :], S.varr, full)
        g.wait_ge(S.sent, n)
        return

    if core in direct or core in proxy:
        slot = items.index(core)
        late_v = None
        if core in direct:
            g.sync.dma_start(T.ks[:], T.k[:, :]).then_inc(S.k, 16)
            v_load(g.scalar)
            idn_n = ones_n = 1
            if core == direct[0]:
                ones_n = count(off)
                identity(g, T)
                exp_table(g, T, T.ramp, S.ramp, 1)
            else:
                constants(g, T)
            v_ones()
            v_fix()
            q_ready = [(S.qarr, count(off))]
            k_ready = [(S.k, 16)]
        else:
            i = proxy.index(core)
            fed = count(topo.mask(far[i], core))
            q_ready = [(S.qarr, count(topo.mask(helper[i], core)))]
            k_ready = [(S.karr, fed)]
            idn_n, ones_n = count(topo.mask(helper[i], core)), fed
            exp_table(g, T, T.ones, S.ones, ones_n)
            v_ones()

            def late_v():
                v_fix(S.varr, fed)
        worker(g, T, q_ready, k_ready, v_done, T.pk[:, 0:129], T.pkm[:, 0:1], idn_n, ones_n, late_v)
        full = count(topo.mask(core, root))
        c0, c1 = CUTS[slot - 1], CUTS[slot]
        g.wait_ge(S.idn, idn_n)
        n = send(root, T.ident[:, c0:c1], T.ident[:, c0:c1], S.idn, full)
        g.wait_ge(S.nm, 1)
        n += send(root, T.mland[:, MW * slot:MW * slot + 1], T.pkm[:, 0:1], S.mA, full)
        g.wait_ge(S.pk, 1)
        n += send(root, T.land[:, W * slot:W * slot + 129], T.pk[:, 0:129], S["ret%d" % slot], full)
        g.wait_ge(S.sent, n)
